import numpy as np
import ml_dtypes


def mxq(x, axis, fmt="e4m3"):
    dtype, down = {"e4m3": (ml_dtypes.float8_e4m3fn, 7), "e5m2": (ml_dtypes.float8_e5m2, 14)}[fmt]
    v = np.moveaxis(np.asarray(x, np.float32).astype(ml_dtypes.bfloat16).astype(np.float64), axis, -1)
    blocks = v.reshape(v.shape[:-1] + (-1, 32))
    amax = np.abs(blocks).max(-1, keepdims=True)
    byte = np.maximum(np.where(amax > 0, np.frexp(amax)[1] - 1 + 127, 0) - down, 1)
    scale = np.exp2(byte - 127.0)
    codes = (blocks / scale).astype(np.float32).astype(dtype).astype(np.float64)
    return np.moveaxis((codes * scale).reshape(v.shape), -1, axis)


WIDE = False


def mx_kscale(k):
    if not WIDE:
        return np.ones(k)
    levels = np.array([10, -10, 5, -5, 0])
    if k % 512:
        return np.exp2(np.random.permutation(np.resize(levels, k // 32))).repeat(32)
    a = np.empty((k // 512, 16))
    for p in range(k // 512):
        a[p, :8] = np.random.permutation(np.resize(levels, 8))
        for g in range(8):
            far = levels[np.abs(levels - a[p, g]) >= 10]
            a[p, g + 8] = far[np.random.randint(len(far))]
    return np.exp2(a.ravel()).repeat(32)


def f64(x):
    return np.asarray(x).astype(np.float64)


def striped(idx):
    return np.tile(np.asarray(idx).reshape(-1, 16).T, (8, 1)).astype(np.uint16)


def unstriped(offs):
    return offs[:16].T.reshape(-1).astype(np.int64)


E2M1 = np.array([0.0, 0.5, 1.0, 1.5, 2.0, 3.0, 4.0, 6.0, -0.0, -0.5, -1.0, -1.5, -2.0, -3.0, -4.0, -6.0])


def pack_weight(w, fmt):
    k, n = w.shape
    w = f64(np.asarray(w, np.float32).astype(ml_dtypes.bfloat16)).reshape(k // 32, 32, n)
    amax = np.abs(w).max(1)
    if fmt == "e4m3":
        byte = np.frexp(amax)[1] - 1 + 127 - 7
    else:
        mant, ex = np.frexp(amax / 6.0)
        byte = np.where(mant > 0.5, ex, ex - 1) + 127
    byte = np.clip(np.where(amax > 0, byte, 1), 1, 254)
    scaled = (w * np.exp2(127.0 - byte)[:, None, :]).reshape(k, n).astype(np.float32)
    by_word = np.ascontiguousarray(scaled.reshape(k // 512, 128, 4, n).transpose(0, 1, 3, 2))
    if fmt == "e4m3":
        words = by_word.astype(ml_dtypes.float8_e4m3fn).view(np.uint8)
    else:
        c = by_word.astype(ml_dtypes.float4_e2m1fn).view(np.uint8) & 0xF
        words = (c[..., 0::2] | (c[..., 1::2] << 4)).reshape(k // 512, 128, 2 * n)
    return np.ascontiguousarray(words), np.ascontiguousarray(byte.astype(np.uint8).reshape(k // 512, 16, n))


def unpack_weight(words, scales, fmt):
    g, _, n = scales.shape
    words = np.ascontiguousarray(words).reshape(g, 128, n, -1)
    if fmt == "e4m3":
        vals = words.view(ml_dtypes.float8_e4m3fn).astype(np.float64)
    else:
        nib = np.empty((g, 128, n, 4), np.uint8)
        nib[..., 0::2] = words & 0xF
        nib[..., 1::2] = words >> 4
        vals = E2M1[nib]
    vals = vals * np.repeat(np.exp2(scales.astype(np.float64) - 127.0), 8, axis=1)[..., None]
    return vals.transpose(0, 1, 3, 2).reshape(g * 512, n)


D, T, I, Q, E, J, U = 512, 2048, 512, 256, 512, 256, 1024


def setup_inputs():
    n = np.random.standard_normal
    idx = np.random.permutation(T)[:I]
    idx2 = np.random.permutation(U)[:J]
    idx3 = np.random.permutation(Q)[:Q]
    fd = mx_kscale(D)
    fi = mx_kscale(I)
    ti = np.ones(T)
    ti[idx] = fi
    keysp = pack_weight(n((D, T)) / fd[:, None], "e4m3")
    return {
        "query": (n((D, Q)) * 0.8 / np.sqrt(D) * fd[:, None]).astype(np.float32),
        "keys_words": keysp[0],
        "keys_scales": keysp[1],
        "kept": (n((D, U)) * 1.5 / np.sqrt(D) * fd[:, None]).astype(np.float32),
        "kw1": (np.random.uniform(0.4, 1.6, (1, J))).astype(np.float32),
        "lam": (np.random.uniform(0.3, 0.7, (1, Q))).astype(np.float32),
        "width": (np.random.uniform(0.3, 0.8, (Q, 1))).astype(np.float32),
        "os": (np.random.uniform(4.0, 16.0, (1, I)) * fi).astype(np.float32),
        "vals": (n((E, T)) / ti).astype(np.float32),
        "hold": (np.random.uniform(0.3, 1.0, (1, Q))).astype(np.float32),
        "offs": striped(idx),
        "offs2": striped(idx2),
        "offs3": striped(idx3),
    }


def reference(query, keys_words, keys_scales, kept, kw1, lam, width, os, vals, hold, offs, offs2, offs3):
    idx = unstriped(offs)
    idx2 = unstriped(offs2)
    idx3 = unstriped(offs3)
    keysu = unpack_weight(keys_words, keys_scales, "e4m3")
    keysidxg = keysu[:, idx]
    queryq = mxq(f64(query), 0, "e4m3")
    a0 = keysidxg.T @ queryq
    keptidx2q = mxq(f64(kept)[:, idx2], 0, "e4m3")
    kk = keysidxg.T @ keptidx2q
    m1 = np.max(kk * f64(kw1), axis=1, keepdims=True)
    s0 = a0 - m1 * f64(lam)
    s = s0.T
    ce = (s - np.mean(s, axis=1, keepdims=True)) / f64(width)
    p = 1.0 / (np.square(ce) + 1.0)
    w = p / np.sum(p, axis=1, keepdims=True)
    wo1 = w * f64(os)
    wt1 = wo1.T
    vt1 = f64(vals)[:, idx].T
    vt1q = mxq(vt1, 0, "e4m3")
    wt1q = mxq(wt1, 0, "e4m3")
    o = vt1q.T @ wt1q
    y = o - o[:, idx3] * f64(hold)
    return y

@@ -1,0 +1,209 @@
+from contextlib import ExitStack
+
+import concourse.mybir as mybir
+from concourse.masks import make_identity
+
+D, T, I, Q, E, J, U = 512, 2048, 512, 256, 512, 256, 1024
+FLOPS = 2 * D * I * Q + 2 * D * I * J + 2 * I * E * Q
+
+F32 = mybir.dt.float32
+BF16 = mybir.dt.bfloat16
+I32 = mybir.dt.int32
+U32 = mybir.dt.uint32
+U16 = mybir.dt.uint16
+U8 = mybir.dt.uint8
+FP8X4 = mybir.dt.float8_e4m3fn_x4
+ALU = mybir.AluOpType
+ACT = mybir.ActivationFunctionType
+AXIS = mybir.AxisListType
+
+P = 128
+PACK = 4
+LANES = 16
+HALF = I // 2
+SPARE = 16
+
+
+def tile_attend_novel_typical_comparedrows_kernel(
+    tc, query, keys_words, keys_scales, kept, kw1, lam, width, slot_factor, vals, hold, offs, offs2, offs3, out
+):
+    nc = tc.nc
+    with ExitStack() as ctx:
+        sb = ctx.enter_context(tc.tile_pool(name="sb", bufs=1))
+        ps = ctx.enter_context(tc.psum_pool(name="ps", bufs=1))
+
+        def bank(tag, shape, name):
+            return ps.tile(shape, F32, tag=tag, name=name)
+
+        def mx(out_ap, lhs, lhs_sc, rhs, rhs_sc):
+            nc.tensor.matmul_mx(out=out_ap, lhsT=lhs.bitcast(FP8X4), lhsT_scale=lhs_sc,
+                                rhs=rhs.bitcast(FP8X4), rhs_scale=rhs_sc, start=True, stop=True)
+
+        def quantize(codes, scales, grouped):
+            nc.vector.quantize_mx(out=codes.bitcast(FP8X4), scales=scales, in_=grouped)
+
+        ident = sb.tile([P, P], F32, name="ident")
+        make_identity(nc, ident[:])
+        list2 = sb.tile([P, J // LANES], U16, name="list2")
+        list1 = sb.tile([P, I // LANES], U16, name="list1")
+        list3 = sb.tile([P, Q // LANES], U16, name="list3")
+        rows = sb.tile([P, P], F32, name="rows")
+        nc.vector.memset(rows[:], 0.0)
+        key_scale_pool = sb.tile([P, T], U8, name="key_scale_pool")
+        nc.vector.memset(key_scale_pool[:].bitcast(I32), 0)
+        width_rows = sb.tile([2, P], F32, name="width_rows")
+        kept_planes = kept.rearrange("(p j) u -> j p u", j=PACK)
+        kept_pool = [sb.tile([P, U], F32, name=f"kept_pool{j}") for j in range(PACK)]
+        nc.sync.dma_start(list2[:], offs2)
+        nc.scalar.dma_start(width_rows[:], width.rearrange("(t p) o -> t (p o)", t=2))
+        for j in range(2):
+            nc.sync.dma_start(kept_pool[j][:], kept_planes[j])
+        nc.sync.dma_start(list1[:], offs)
+        nc.scalar.dma_start(rows[2:4, :], kw1.rearrange("o (t p) -> t (o p)", t=2))
+        nc.scalar.dma_start(rows[4:6, :], lam.rearrange("o (t p) -> t (o p)", t=2))
+        nc.scalar.dma_start(rows[8:12, :], slot_factor.rearrange("o (t p) -> t (o p)", t=4))
+        nc.scalar.dma_start(rows[6:8, :], hold.rearrange("o (t p) -> t (o p)", t=2))
+        for r in range(4):
+            nc.scalar.dma_start(key_scale_pool[r:P:32, :].bitcast(I32), keys_scales[0, r:16:4, :].bitcast(I32))
+        for j in range(2, PACK):
+            nc.sync.dma_start(kept_pool[j][:], kept_planes[j])
+        key_word_pool = sb.tile([P, T], U32, name="key_word_pool")
+        nc.sync.dma_start(key_word_pool[:].bitcast(I32), keys_words[0].rearrange("p n t -> p (n t)").bitcast(I32))
+        query_raw = sb.tile([P, PACK, Q], F32, name="query_raw")
+        nc.sync.dma_start(query_raw[:], query.rearrange("(p j) q -> p j q", j=PACK))
+        val_pool = [sb.tile([P, T], F32, name=f"val_pool{e}") for e in range(E // P)]
+        for e in range(E // P):
+            nc.sync.dma_start(val_pool[e][:], vals[e * P:(e + 1) * P, :])
+        nc.sync.dma_start(list3[:], offs3)
+
+        nc.scalar.activation(rows[0:2, :], width_rows[:], ACT.Abs_reciprocal_sqrt)
+        rows_t = bank("b0", [P, P], "rows_t")
+        nc.tensor.transpose(rows_t[:], rows[:], ident[:])
+        cols = sb.tile([P, 12], F32, name="cols")
+        nc.vector.tensor_copy(cols[:], rows_t[:, 0:12])
+        inv_width = sb.tile([P, 2], F32, name="inv_width")
+        nc.vector.tensor_tensor(inv_width[:], cols[:, 0:2], cols[:, 0:2], ALU.mult)
+        square_scale = sb.tile([P, 2], F32, name="square_scale")
+        nc.vector.scalar_tensor_tensor(square_scale[:], inv_width[:], 1.0 / (I * I), inv_width[:], ALU.mult, ALU.mult)
+        os_rows = bank("b5", [P, I], "os_rows")
+        for t in range(I // P):
+            nc.tensor.transpose(os_rows[:, t * P:(t + 1) * P], cols[:, 8 + t:9 + t].to_broadcast([P, P]), ident[:])
+        hold_bank = bank("b1", [P, Q], "hold_bank")
+        for t in range(Q // P):
+            nc.tensor.transpose(hold_bank[:, t * P:(t + 1) * P], cols[:, 6 + t:7 + t].to_broadcast([P, P]), ident[:])
+        hold_rows = sb.tile([P, Q], F32, name="hold_rows")
+        nc.scalar.copy(hold_rows[:], hold_bank[:])
+
+        kept_picked = sb.tile([P, PACK, J], BF16, name="kept_picked")
+        for j in range(PACK):
+            nc.scalar.activation(kept_picked[:, j, :], kept_pool[j][:].indirect(list2[:]), ACT.Copy)
+        key_scales = sb.tile([P, I], U8, name="key_scales", align_bytes=64)
+        nc.vector.tensor_copy(key_scales[:], key_scale_pool[:].indirect(list1[:]))
+        kept_grouped = sb.tile([P, J, PACK], BF16, name="kept_grouped", align_bytes=64)
+        nc.vector.tensor_copy(kept_grouped[:], kept_picked[:].rearrange("p j c -> p c j"))
+        kept_codes = sb.tile([P, J], U32, name="kept_codes", align_bytes=64)
+        kept_scales = sb.tile([P, J], U8, name="kept_scales", align_bytes=64)
+        quantize(kept_codes[:], kept_scales[:], kept_grouped[:].rearrange("p c j -> p (c j)"))
+
+        key_words = sb.tile([P, I], U32, name="key_words", align_bytes=64)
+        for h in range(2):
+            nc.vector.tensor_copy(key_words[:, h * HALF:(h + 1) * HALF],
+                                  key_word_pool[:].indirect(list1[:, h * (HALF // LANES):(h + 1) * (HALF // LANES)]))
+        query_grouped = sb.tile([P, Q, PACK], BF16, name="query_grouped", align_bytes=64)
+        query_codes = sb.tile([P, Q], U32, name="query_codes", align_bytes=64)
+        query_scales = sb.tile([P, Q], U8, name="query_scales", align_bytes=64)
+        m1_cols = sb.tile([P, I // P], F32, name="m1_cols")
+        kk, largest = [], []
+        for h in range(2):
+            slots = slice(h * HALF, (h + 1) * HALF)
+            kk.append(bank(f"b{h}", [P, 2, HALF], f"kk{h}"))
+            for t in range(2):
+                mx(kk[h][:, t, :], kept_codes[:, t * P:(t + 1) * P], kept_scales[:, t * P:(t + 1) * P],
+                   key_words[:, slots], key_scales[:, slots])
+        nc.vector.tensor_copy(query_grouped[:].rearrange("p (c i) j -> p c j i", i=4),
+                              query_raw[:].rearrange("p j (c i) -> p c j i", i=4))
+        for h in range(2):
+            first = sb.tile([P, HALF], F32, name=f"first{h}")
+            nc.scalar.activation(first[:], kk[h][:, 0, :], ACT.Copy, scale=cols[:, 2:3])
+            largest.append(sb.tile([P, HALF], F32, name=f"largest{h}"))
+            nc.vector.scalar_tensor_tensor(largest[h][:], kk[h][:, 1, :], cols[:, 3:4], first[:], ALU.mult, ALU.max)
+        quantize(query_codes[:], query_scales[:], query_grouped[:].rearrange("p c j -> p (c j)"))
+        for h in range(2):
+            turned = bank(f"b{h}", [P, 2, P], f"turned{h}")
+            for t in range(2):
+                nc.tensor.transpose(turned[:, t, :], largest[h][:, t * P:(t + 1) * P], ident[:])
+            nc.vector.tensor_reduce(m1_cols[:, 2 * h:2 * h + 2], turned[:], AXIS.X, ALU.max)
+        a0 = []
+        for t in range(2):
+            a0_bank = bank(f"b{2 + t}", [P, I], f"a0_bank{t}")
+            mx(a0_bank[:], query_codes[:, t * P:(t + 1) * P], query_scales[:, t * P:(t + 1) * P], key_words[:], key_scales[:])
+            a0.append(sb.tile([P, I], F32, name=f"a0_{t}"))
+            nc.scalar.copy(a0[t][:], a0_bank[:])
+        m1_rows = bank("b4", [P, I], "m1_rows")
+        for t in range(I // P):
+            nc.tensor.transpose(m1_rows[:, t * P:(t + 1) * P], m1_cols[:, t:t + 1].to_broadcast([P, P]), ident[:])
+
+        weight_grouped = sb.tile([P, Q, PACK], BF16, name="weight_grouped", align_bytes=64)
+        weight_codes = sb.tile([P, Q], U32, name="weight_codes", align_bytes=64)
+        weight_scales = sb.tile([P, Q], U8, name="weight_scales", align_bytes=64)
+        minus_s, s_sum, root = [], [], []
+        for t in range(2):
+            minus_s.append(sb.tile([P, I], F32, name=f"minus_s{t}"))
+            s_sum.append(sb.tile([P, 1], F32, name=f"s_sum{t}"))
+            nc.vector.scalar_tensor_tensor(minus_s[t][:], m1_rows[:], cols[:, 4 + t:5 + t], a0[t][:],
+                                           ALU.mult, ALU.subtract, accum_out=s_sum[t][:])
+        for t in range(2):
+            square = sb.tile([P, I], F32, name=f"square{t}")
+            nc.scalar.activation(square[:], minus_s[t][:], ACT.Square, scale=-float(I), bias=s_sum[t][:])
+            root.append(sb.tile([P, I], F32, name=f"root{t}"))
+            nc.scalar.activation(root[t][:], square[:], ACT.Abs_reciprocal_sqrt, scale=square_scale[:, t:t + 1], bias=1.0)
+        for t in range(2):
+            part = sb.tile([P, I], F32, name=f"part{t}")
+            part_sum = sb.tile([P, 1], F32, name=f"part_sum{t}")
+            if t == 0:
+                nc.vector.scalar_tensor_tensor(part[:], root[t][:], 1.0, root[t][:], ALU.mult, ALU.mult, accum_out=part_sum[:])
+            else:
+                nc.scalar.activation(part[:], root[t][:], ACT.Square, accum_out=part_sum[:])
+            inv_sum = sb.tile([P, 1], F32, name=f"inv_sum{t}")
+            nc.vector.reciprocal(inv_sum[:], part_sum[:])
+            weight = sb.tile([P, I], BF16, name=f"weight{t}")
+            nc.vector.scalar_tensor_tensor(weight[:], part[:], inv_sum[:], os_rows[:], ALU.mult, ALU.mult)
+            weight_t = bank(f"b{2 + t}", [P, 2, P], f"weight_t{t}")
+            words = weight[:].bitcast(F32)
+            for u in range(2):
+                nc.tensor.transpose(weight_t[:, u, :], words[:, u:I // 2:2], ident[:])
+            rows_t_cols = slice(t * P, (t + 1) * P)
+            nc.scalar.copy(weight_grouped[:, rows_t_cols, :].bitcast(F32), weight_t[:].rearrange("p u q -> p q u"))
+            quantize(weight_codes[:, rows_t_cols], weight_scales[:, rows_t_cols],
+                     weight_grouped[:, rows_t_cols, :].rearrange("p c j -> p (c j)"))
+
+        val_codes, val_scales = [], []
+        for e in range(E // P):
+            picked = sb.tile([P, I], BF16, name=f"val_picked{e}")
+            for h in range(2):
+                window = val_pool[e][:].indirect(list1[:, h * (HALF // LANES):(h + 1) * (HALF // LANES)])
+                if h == 0:
+                    nc.scalar.activation(picked[:, h * HALF:(h + 1) * HALF], window, ACT.Copy)
+                else:
+                    nc.vector.tensor_copy(picked[:, h * HALF:(h + 1) * HALF], window)
+            val_t = bank(f"b{6 + e % 2}", [P, 2, P], f"val_t{e}")
+            words = picked[:].bitcast(F32)
+            for u in range(2):
+                nc.tensor.transpose(val_t[:, u, :], words[:, u:I // 2:2], ident[:])
+            grouped = sb.tile([P, P, PACK], BF16, name=f"val_grouped{e}", align_bytes=64)
+            nc.scalar.copy(grouped[:].bitcast(F32), val_t[:].rearrange("p u c -> p c u"))
+            val_codes.append(sb.tile([P, P], U32, name=f"val_codes{e}", align_bytes=64))
+            val_scales.append(sb.tile([P, P], U8, name=f"val_scales{e}", align_bytes=64))
+            quantize(val_codes[e][:], val_scales[e][:], grouped[:].rearrange("p c j -> p (c j)"))
+
+        for e in range(E // P):
+            o_bank = bank(("b2", "b3", "b4", "b0")[e], [P, Q], f"o_bank{e}")
+            mx(o_bank[:], val_codes[e][:], val_scales[e][:], weight_codes[:], weight_scales[:])
+            o_window = sb.tile([P, Q + SPARE], F32, name=f"o_window{e}")
+            nc.gpsimd.memset(o_window[:, Q:], 0.0)
+            nc.scalar.copy(o_window[:, :Q], o_bank[:])
+            taken = sb.tile([P, Q], F32, name=f"taken{e}")
+            nc.vector.tensor_tensor(taken[:], o_window[:].indirect(list3[:]), hold_rows[:], ALU.mult)
+            result = sb.tile([P, Q], F32, name=f"result{e}")
+            nc.vector.tensor_tensor(result[:], o_bank[:], taken[:], ALU.subtract)
+            nc.sync.dma_start(out[e * P:(e + 1) * P, :], result[:])

@@ -42,76 +42,95 @@ def tile_attend_novel_typical_comparedrows_kernel(
         def quantize(codes, scales, grouped):
             nc.vector.quantize_mx(out=codes.bitcast(FP8X4), scales=scales, in_=grouped)
 
+        key_scale_pool = sb.tile([P, T], U8, name="key_scale_pool")
+        nc.gpsimd.memset(key_scale_pool[:].bitcast(I32), 0)
+        rows = sb.tile([P, P], F32, name="rows")
+        nc.gpsimd.memset(rows[:], 0.0)
+        late_rows = sb.tile([P, P], F32, name="late_rows")
+        nc.gpsimd.memset(late_rows[:], 0.0)
+        nc.gpsimd.dma_start(late_rows[0:2, :], lam.rearrange("o (t p) -> t (o p)", t=2))
+        nc.gpsimd.dma_start(late_rows[4:8, :], slot_factor.rearrange("o (t p) -> t (o p)", t=4))
+        nc.gpsimd.dma_start(late_rows[2:4, :], hold.rearrange("o (t p) -> t (o p)", t=2))
         ident = sb.tile([P, P], F32, name="ident")
         make_identity(nc, ident[:])
         list2 = sb.tile([P, J // LANES], U16, name="list2")
         list1 = sb.tile([P, I // LANES], U16, name="list1")
         list3 = sb.tile([P, Q // LANES], U16, name="list3")
-        rows = sb.tile([P, P], F32, name="rows")
-        nc.vector.memset(rows[:], 0.0)
-        key_scale_pool = sb.tile([P, T], U8, name="key_scale_pool")
-        nc.vector.memset(key_scale_pool[:].bitcast(I32), 0)
-        width_rows = sb.tile([2, P], F32, name="width_rows")
-        kept_planes = kept.rearrange("(p j) u -> j p u", j=PACK)
-        kept_pool = [sb.tile([P, U], F32, name=f"kept_pool{j}") for j in range(PACK)]
+        width_rows = sb.tile([2, P], F32, name="width_rows", tag="load3")
+        kept_planes = kept.rearrange("(p j) u -> p j u", j=PACK)
+        kept_pool = [sb.tile([P, 2, U], F32, name=f"kept_pool{g}", tag=f"load{g}") for g in range(2)]
         nc.sync.dma_start(list2[:], offs2)
         nc.scalar.dma_start(width_rows[:], width.rearrange("(t p) o -> t (p o)", t=2))
-        for j in range(2):
-            nc.sync.dma_start(kept_pool[j][:], kept_planes[j])
         nc.sync.dma_start(list1[:], offs)
-        nc.scalar.dma_start(rows[2:4, :], kw1.rearrange("o (t p) -> t (o p)", t=2))
-        nc.scalar.dma_start(rows[4:6, :], lam.rearrange("o (t p) -> t (o p)", t=2))
-        nc.scalar.dma_start(rows[8:12, :], slot_factor.rearrange("o (t p) -> t (o p)", t=4))
-        nc.scalar.dma_start(rows[6:8, :], hold.rearrange("o (t p) -> t (o p)", t=2))
-        for r in range(4):
-            nc.scalar.dma_start(key_scale_pool[r:P:32, :].bitcast(I32), keys_scales[0, r:16:4, :].bitcast(I32))
-        for j in range(2, PACK):
-            nc.sync.dma_start(kept_pool[j][:], kept_planes[j])
-        key_word_pool = sb.tile([P, T], U32, name="key_word_pool")
-        nc.sync.dma_start(key_word_pool[:].bitcast(I32), keys_words[0].rearrange("p n t -> p (n t)").bitcast(I32))
         query_raw = sb.tile([P, PACK, Q], F32, name="query_raw")
         nc.sync.dma_start(query_raw[:], query.rearrange("(p j) q -> p j q", j=PACK))
-        val_pool = [sb.tile([P, T], F32, name=f"val_pool{e}") for e in range(E // P)]
-        for e in range(E // P):
-            nc.sync.dma_start(val_pool[e][:], vals[e * P:(e + 1) * P, :])
+        for g in range(2):
+            nc.sync.dma_start(kept_pool[g][:], kept_planes[:, 2 * g:2 * g + 2, :])
         nc.sync.dma_start(list3[:], offs3)
+        for r in range(4):
+            nc.scalar.dma_start(key_scale_pool[r:P:32, :].bitcast(I32), keys_scales[0, r:16:4, :].bitcast(I32))
+        nc.scalar.dma_start(rows[2:4, :], kw1.rearrange("o (t p) -> t (o p)", t=2))
+        root_rows = sb.tile([2, P], F32, name="root_rows")
+        nc.scalar.activation(root_rows[:], width_rows[:], ACT.Abs_reciprocal_sqrt)
+        nc.scalar.activation(rows[0:2, :], root_rows[:], ACT.Square)
+        key_word_pool = sb.tile([P, T], U32, name="key_word_pool", tag="load3")
+        nc.sync.dma_start(key_word_pool[:].bitcast(I32), keys_words[0].rearrange("p n t -> p (n t)").bitcast(I32))
 
-        nc.scalar.activation(rows[0:2, :], width_rows[:], ACT.Abs_reciprocal_sqrt)
+        query_grouped = sb.tile([P, Q, PACK], BF16, name="query_grouped", align_bytes=64)
+        query_codes = sb.tile([P, Q], U32, name="query_codes", align_bytes=64)
+        query_scales = sb.tile([P, Q], U8, name="query_scales", align_bytes=64)
+        nc.vector.tensor_copy(query_grouped[:].rearrange("p (c i) j -> p c j i", i=4),
+                              query_raw[:].rearrange("p j (c i) -> p c j i", i=4))
+        quantize(query_codes[:], query_scales[:], query_grouped[:].rearrange("p c j -> p (c j)"))
+
         rows_t = bank("b0", [P, P], "rows_t")
         nc.tensor.transpose(rows_t[:], rows[:], ident[:])
-        cols = sb.tile([P, 12], F32, name="cols")
-        nc.vector.tensor_copy(cols[:], rows_t[:, 0:12])
-        inv_width = sb.tile([P, 2], F32, name="inv_width")
-        nc.vector.tensor_tensor(inv_width[:], cols[:, 0:2], cols[:, 0:2], ALU.mult)
+        cols = sb.tile([P, 4], F32, name="cols")
+        nc.vector.tensor_copy(cols[:], rows_t[:, 0:4])
         square_scale = sb.tile([P, 2], F32, name="square_scale")
-        nc.vector.scalar_tensor_tensor(square_scale[:], inv_width[:], 1.0 / (I * I), inv_width[:], ALU.mult, ALU.mult)
+        nc.vector.scalar_tensor_tensor(square_scale[:], cols[:, 0:2], 1.0 / (I * I), cols[:, 0:2], ALU.mult, ALU.mult)
+        late_t = bank("b4", [P, P], "late_t")
+        nc.tensor.transpose(late_t[:], late_rows[:], ident[:])
+        late_cols = sb.tile([P, 8], F32, name="late_cols")
+        nc.scalar.copy(late_cols[:], late_t[:, 0:8])
         os_rows = bank("b5", [P, I], "os_rows")
         for t in range(I // P):
-            nc.tensor.transpose(os_rows[:, t * P:(t + 1) * P], cols[:, 8 + t:9 + t].to_broadcast([P, P]), ident[:])
-        hold_bank = bank("b1", [P, Q], "hold_bank")
+            nc.tensor.transpose(os_rows[:, t * P:(t + 1) * P], late_cols[:, 4 + t:5 + t].to_broadcast([P, P]), ident[:])
+        hold_bank = bank("b6", [P, Q], "hold_bank")
         for t in range(Q // P):
-            nc.tensor.transpose(hold_bank[:, t * P:(t + 1) * P], cols[:, 6 + t:7 + t].to_broadcast([P, P]), ident[:])
+            nc.tensor.transpose(hold_bank[:, t * P:(t + 1) * P], late_cols[:, 2 + t:3 + t].to_broadcast([P, P]), ident[:])
         hold_rows = sb.tile([P, Q], F32, name="hold_rows")
         nc.scalar.copy(hold_rows[:], hold_bank[:])
 
-        kept_picked = sb.tile([P, PACK, J], BF16, name="kept_picked")
+        kept_picked = sb.tile([P, PACK, J], F32, name="kept_picked")
         for j in range(PACK):
-            nc.scalar.activation(kept_picked[:, j, :], kept_pool[j][:].indirect(list2[:]), ACT.Copy)
+            window = kept_pool[j // 2][:, j % 2, :].indirect(list2[:])
+            if j % 2 == 0:
+                nc.scalar.activation(kept_picked[:, j, :], window, ACT.Copy)
+            else:
+                nc.vector.tensor_copy(kept_picked[:, j, :], window)
         key_scales = sb.tile([P, I], U8, name="key_scales", align_bytes=64)
         nc.vector.tensor_copy(key_scales[:], key_scale_pool[:].indirect(list1[:]))
         kept_grouped = sb.tile([P, J, PACK], BF16, name="kept_grouped", align_bytes=64)
-        nc.vector.tensor_copy(kept_grouped[:], kept_picked[:].rearrange("p j c -> p c j"))
+        nc.vector.tensor_copy(kept_grouped[:].rearrange("p (c i) j -> p c j i", i=4),
+                              kept_picked[:].rearrange("p j (c i) -> p c j i", i=4))
         kept_codes = sb.tile([P, J], U32, name="kept_codes", align_bytes=64)
         kept_scales = sb.tile([P, J], U8, name="kept_scales", align_bytes=64)
         quantize(kept_codes[:], kept_scales[:], kept_grouped[:].rearrange("p c j -> p (c j)"))
+        val_pool = []
+
+        def load_values(e, tag):
+            val_pool.append(sb.tile([P, T], F32, name=f"val_pool{e}", tag=tag))
+            nc.sync.dma_start(val_pool[e][:], vals[e * P:(e + 1) * P, :])
+
+        for e in range(2):
+            load_values(e, f"load{e}")
 
         key_words = sb.tile([P, I], U32, name="key_words", align_bytes=64)
         for h in range(2):
             nc.vector.tensor_copy(key_words[:, h * HALF:(h + 1) * HALF],
                                   key_word_pool[:].indirect(list1[:, h * (HALF // LANES):(h + 1) * (HALF // LANES)]))
-        query_grouped = sb.tile([P, Q, PACK], BF16, name="query_grouped", align_bytes=64)
-        query_codes = sb.tile([P, Q], U32, name="query_codes", align_bytes=64)
-        query_scales = sb.tile([P, Q], U8, name="query_scales", align_bytes=64)
+        load_values(2, "load3")
         m1_cols = sb.tile([P, I // P], F32, name="m1_cols")
         kk, largest = [], []
         for h in range(2):
@@ -120,14 +139,12 @@ def tile_attend_novel_typical_comparedrows_kernel(
             for t in range(2):
                 mx(kk[h][:, t, :], kept_codes[:, t * P:(t + 1) * P], kept_scales[:, t * P:(t + 1) * P],
                    key_words[:, slots], key_scales[:, slots])
-        nc.vector.tensor_copy(query_grouped[:].rearrange("p (c i) j -> p c j i", i=4),
-                              query_raw[:].rearrange("p j (c i) -> p c j i", i=4))
         for h in range(2):
-            first = sb.tile([P, HALF], F32, name=f"first{h}")
+            first = sb.tile([P, HALF], F32, name=f"first{h}", tag=f"first{h}")
             nc.scalar.activation(first[:], kk[h][:, 0, :], ACT.Copy, scale=cols[:, 2:3])
-            largest.append(sb.tile([P, HALF], F32, name=f"largest{h}"))
+            largest.append(sb.tile([P, HALF], F32, name=f"largest{h}", tag=f"largest{h}"))
             nc.vector.scalar_tensor_tensor(largest[h][:], kk[h][:, 1, :], cols[:, 3:4], first[:], ALU.mult, ALU.max)
-        quantize(query_codes[:], query_scales[:], query_grouped[:].rearrange("p c j -> p (c j)"))
+        load_values(3, "first1")
         for h in range(2):
             turned = bank(f"b{h}", [P, 2, P], f"turned{h}")
             for t in range(2):
@@ -137,11 +154,12 @@ def tile_attend_novel_typical_comparedrows_kernel(
         for t in range(2):
             a0_bank = bank(f"b{2 + t}", [P, I], f"a0_bank{t}")
             mx(a0_bank[:], query_codes[:, t * P:(t + 1) * P], query_scales[:, t * P:(t + 1) * P], key_words[:], key_scales[:])
-            a0.append(sb.tile([P, I], F32, name=f"a0_{t}"))
+            a0.append(sb.tile([P, I], F32, name=f"a0_{t}", tag=f"a0_{t}"))
             nc.scalar.copy(a0[t][:], a0_bank[:])
         m1_rows = bank("b4", [P, I], "m1_rows")
         for t in range(I // P):
             nc.tensor.transpose(m1_rows[:, t * P:(t + 1) * P], m1_cols[:, t:t + 1].to_broadcast([P, P]), ident[:])
+
 
         weight_grouped = sb.tile([P, Q, PACK], BF16, name="weight_grouped", align_bytes=64)
         weight_codes = sb.tile([P, Q], U32, name="weight_codes", align_bytes=64)
@@ -150,15 +168,15 @@ def tile_attend_novel_typical_comparedrows_kernel(
         for t in range(2):
             minus_s.append(sb.tile([P, I], F32, name=f"minus_s{t}"))
             s_sum.append(sb.tile([P, 1], F32, name=f"s_sum{t}"))
-            nc.vector.scalar_tensor_tensor(minus_s[t][:], m1_rows[:], cols[:, 4 + t:5 + t], a0[t][:],
+            nc.vector.scalar_tensor_tensor(minus_s[t][:], m1_rows[:], late_cols[:, t:t + 1], a0[t][:],
                                            ALU.mult, ALU.subtract, accum_out=s_sum[t][:])
         for t in range(2):
-            square = sb.tile([P, I], F32, name=f"square{t}")
+            square = sb.tile([P, I], F32, name=f"square{t}", tag=f"square{t}")
             nc.scalar.activation(square[:], minus_s[t][:], ACT.Square, scale=-float(I), bias=s_sum[t][:])
-            root.append(sb.tile([P, I], F32, name=f"root{t}"))
+            root.append(sb.tile([P, I], F32, name=f"root{t}", tag=f"root{t}"))
             nc.scalar.activation(root[t][:], square[:], ACT.Abs_reciprocal_sqrt, scale=square_scale[:, t:t + 1], bias=1.0)
         for t in range(2):
-            part = sb.tile([P, I], F32, name=f"part{t}")
+            part = sb.tile([P, I], F32, name=f"part{t}", tag=f"part{t}")
             part_sum = sb.tile([P, 1], F32, name=f"part_sum{t}")
             if t == 0:
                 nc.vector.scalar_tensor_tensor(part[:], root[t][:], 1.0, root[t][:], ALU.mult, ALU.mult, accum_out=part_sum[:])
@@ -173,19 +191,21 @@ def tile_attend_novel_typical_comparedrows_kernel(
             for u in range(2):
                 nc.tensor.transpose(weight_t[:, u, :], words[:, u:I // 2:2], ident[:])
             rows_t_cols = slice(t * P, (t + 1) * P)
-            nc.scalar.copy(weight_grouped[:, rows_t_cols, :].bitcast(F32), weight_t[:].rearrange("p u q -> p q u"))
+            leave_bank = nc.scalar.copy if t == 0 else nc.vector.tensor_copy
+            leave_bank(weight_grouped[:, rows_t_cols, :].bitcast(F32), weight_t[:].rearrange("p u q -> p q u"))
             quantize(weight_codes[:, rows_t_cols], weight_scales[:, rows_t_cols],
                      weight_grouped[:, rows_t_cols, :].rearrange("p c j -> p (c j)"))
 
         val_codes, val_scales = [], []
         for e in range(E // P):
-            picked = sb.tile([P, I], BF16, name=f"val_picked{e}")
-            for h in range(2):
-                window = val_pool[e][:].indirect(list1[:, h * (HALF // LANES):(h + 1) * (HALF // LANES)])
-                if h == 0:
-                    nc.scalar.activation(picked[:, h * HALF:(h + 1) * HALF], window, ACT.Copy)
-                else:
-                    nc.vector.tensor_copy(picked[:, h * HALF:(h + 1) * HALF], window)
+            picked = sb.tile([P, I], BF16, name=f"val_picked{e}", tag=("largest1", "a0_1", "root1", "part1")[e])
+            if e == 0:
+                nc.scalar.activation(picked[:, :HALF], val_pool[e][:].indirect(list1[:, :HALF // LANES]), ACT.Copy)
+                nc.vector.tensor_copy(picked[:, HALF:], val_pool[e][:].indirect(list1[:, HALF // LANES:]))
+            elif e == 1:
+                nc.vector.tensor_copy(picked[:], val_pool[e][:].indirect(list1[:]))
+            else:
+                nc.scalar.activation(picked[:], val_pool[e][:].indirect(list1[:]), ACT.Copy)
             val_t = bank(f"b{6 + e % 2}", [P, 2, P], f"val_t{e}")
             words = picked[:].bitcast(F32)
             for u in range(2):
@@ -203,7 +223,12 @@ def tile_attend_novel_typical_comparedrows_kernel(
             nc.gpsimd.memset(o_window[:, Q:], 0.0)
             nc.scalar.copy(o_window[:, :Q], o_bank[:])
             taken = sb.tile([P, Q], F32, name=f"taken{e}")
-            nc.vector.tensor_tensor(taken[:], o_window[:].indirect(list3[:]), hold_rows[:], ALU.mult)
+            if e == 2:
+                named = sb.tile([P, Q], F32, name="named")
+                nc.scalar.activation(named[:], o_window[:].indirect(list3[:]), ACT.Copy)
+                nc.vector.tensor_tensor(taken[:], named[:], hold_rows[:], ALU.mult)
+            else:
+                nc.vector.tensor_tensor(taken[:], o_window[:].indirect(list3[:]), hold_rows[:], ALU.mult)
             result = sb.tile([P, Q], F32, name=f"result{e}")
             nc.vector.tensor_tensor(result[:], o_bank[:], taken[:], ALU.subtract)
             nc.sync.dma_start(out[e * P:(e + 1) * P, :], result[:])

@@ -44,65 +44,47 @@ def tile_attend_novel_typical_comparedrows_kernel(
 
         key_scale_pool = sb.tile([P, T], U8, name="key_scale_pool")
         nc.gpsimd.memset(key_scale_pool[:].bitcast(I32), 0)
-        rows = sb.tile([P, P], F32, name="rows")
+        rows = sb.tile([P, P], F32, name="rows", tag="late")
         nc.gpsimd.memset(rows[:], 0.0)
-        late_rows = sb.tile([P, P], F32, name="late_rows")
-        nc.gpsimd.memset(late_rows[:], 0.0)
-        nc.gpsimd.dma_start(late_rows[0:2, :], lam.rearrange("o (t p) -> t (o p)", t=2))
-        nc.gpsimd.dma_start(late_rows[4:8, :], slot_factor.rearrange("o (t p) -> t (o p)", t=4))
-        nc.gpsimd.dma_start(late_rows[2:4, :], hold.rearrange("o (t p) -> t (o p)", t=2))
         ident = sb.tile([P, P], F32, name="ident")
         make_identity(nc, ident[:])
         list2 = sb.tile([P, J // LANES], U16, name="list2")
         list1 = sb.tile([P, I // LANES], U16, name="list1")
         list3 = sb.tile([P, Q // LANES], U16, name="list3")
-        width_rows = sb.tile([2, P], F32, name="width_rows", tag="load3")
+        width_rows = sb.tile([2, P], F32, name="width_rows", tag="load1", align_bytes=64)
         kept_planes = kept.rearrange("(p j) u -> p j u", j=PACK)
-        kept_pool = [sb.tile([P, 2, U], F32, name=f"kept_pool{g}", tag=f"load{g}") for g in range(2)]
+        kept_pool = [sb.tile([P, 2, U], F32, name="kept_pool0", tag="load0", align_bytes=64)]
         nc.sync.dma_start(list2[:], offs2)
         nc.scalar.dma_start(width_rows[:], width.rearrange("(t p) o -> t (p o)", t=2))
         nc.sync.dma_start(list1[:], offs)
-        query_raw = sb.tile([P, PACK, Q], F32, name="query_raw")
-        nc.sync.dma_start(query_raw[:], query.rearrange("(p j) q -> p j q", j=PACK))
-        for g in range(2):
-            nc.sync.dma_start(kept_pool[g][:], kept_planes[:, 2 * g:2 * g + 2, :])
         nc.sync.dma_start(list3[:], offs3)
+        nc.sync.dma_start(kept_pool[0][:], kept_planes[:, 0:2, :])
         for r in range(4):
-            nc.scalar.dma_start(key_scale_pool[r:P:32, :].bitcast(I32), keys_scales[0, r:16:4, :].bitcast(I32))
-        nc.scalar.dma_start(rows[2:4, :], kw1.rearrange("o (t p) -> t (o p)", t=2))
-        root_rows = sb.tile([2, P], F32, name="root_rows")
+            nc.sync.dma_start(key_scale_pool[r:P:32, :].bitcast(I32), keys_scales[0, r:16:4, :].bitcast(I32))
+        nc.sync.dma_start(rows[2:4, :], kw1.rearrange("o (t p) -> t (o p)", t=2))
+        nc.sync.dma_start(rows[4:6, :], lam.rearrange("o (t p) -> t (o p)", t=2))
+        root_rows = sb.tile([2, P], F32, name="root_rows", tag="load2", align_bytes=64)
         nc.scalar.activation(root_rows[:], width_rows[:], ACT.Abs_reciprocal_sqrt)
-        nc.scalar.activation(rows[0:2, :], root_rows[:], ACT.Square)
+        inverse_rows = sb.tile([2, P], F32, name="inverse_rows", tag="load3")
+        nc.scalar.activation(inverse_rows[:], root_rows[:], ACT.Square)
+        nc.scalar.activation(rows[0:2, :], inverse_rows[:], ACT.Square, scale=1.0 / I)
+        kept_pool.append(sb.tile([P, 2, U], F32, name="kept_pool1", tag="load1", align_bytes=64))
+        nc.sync.dma_start(kept_pool[1][:], kept_planes[:, 2:4, :])
+        query_raw = sb.tile([P, PACK, Q], F32, name="query_raw", tag="load2", align_bytes=64)
+        nc.sync.dma_start(query_raw[:], query.rearrange("(p j) q -> p j q", j=PACK))
         key_word_pool = sb.tile([P, T], U32, name="key_word_pool", tag="load3")
         nc.sync.dma_start(key_word_pool[:].bitcast(I32), keys_words[0].rearrange("p n t -> p (n t)").bitcast(I32))
 
-        query_grouped = sb.tile([P, Q, PACK], BF16, name="query_grouped", align_bytes=64)
-        query_codes = sb.tile([P, Q], U32, name="query_codes", align_bytes=64)
-        query_scales = sb.tile([P, Q], U8, name="query_scales", align_bytes=64)
-        nc.vector.tensor_copy(query_grouped[:].rearrange("p (c i) j -> p c j i", i=4),
-                              query_raw[:].rearrange("p j (c i) -> p c j i", i=4))
-        quantize(query_codes[:], query_scales[:], query_grouped[:].rearrange("p c j -> p (c j)"))
-
         rows_t = bank("b0", [P, P], "rows_t")
         nc.tensor.transpose(rows_t[:], rows[:], ident[:])
-        cols = sb.tile([P, 4], F32, name="cols")
-        nc.vector.tensor_copy(cols[:], rows_t[:, 0:4])
-        square_scale = sb.tile([P, 2], F32, name="square_scale")
-        nc.vector.scalar_tensor_tensor(square_scale[:], cols[:, 0:2], 1.0 / (I * I), cols[:, 0:2], ALU.mult, ALU.mult)
-        late_t = bank("b4", [P, P], "late_t")
-        nc.tensor.transpose(late_t[:], late_rows[:], ident[:])
-        late_cols = sb.tile([P, 8], F32, name="late_cols")
-        nc.scalar.copy(late_cols[:], late_t[:, 0:8])
-        os_rows = bank("b5", [P, I], "os_rows")
-        for t in range(I // P):
-            nc.tensor.transpose(os_rows[:, t * P:(t + 1) * P], late_cols[:, 4 + t:5 + t].to_broadcast([P, P]), ident[:])
-        hold_bank = bank("b6", [P, Q], "hold_bank")
-        for t in range(Q // P):
-            nc.tensor.transpose(hold_bank[:, t * P:(t + 1) * P], late_cols[:, 2 + t:3 + t].to_broadcast([P, P]), ident[:])
-        hold_rows = sb.tile([P, Q], F32, name="hold_rows")
-        nc.scalar.copy(hold_rows[:], hold_bank[:])
+        late_rows = sb.tile([P, P], F32, name="late_rows", tag="late")
+        nc.gpsimd.memset(late_rows[:], 0.0)
+        nc.sync.dma_start(late_rows[0:4, :], slot_factor.rearrange("o (t p) -> t (o p)", t=4))
+        nc.sync.dma_start(late_rows[4:6, :], hold.rearrange("o (t p) -> t (o p)", t=2))
+        cols = sb.tile([P, 6], F32, name="cols")
+        nc.scalar.copy(cols[:], rows_t[:, 0:6])
 
-        kept_picked = sb.tile([P, PACK, J], F32, name="kept_picked")
+        kept_picked = sb.tile([P, PACK, J], F32, name="kept_picked", tag="load4", align_bytes=64)
         for j in range(PACK):
             window = kept_pool[j // 2][:, j % 2, :].indirect(list2[:])
             if j % 2 == 0:
@@ -112,25 +94,33 @@ def tile_attend_novel_typical_comparedrows_kernel(
         key_scales = sb.tile([P, I], U8, name="key_scales", align_bytes=64)
         nc.vector.tensor_copy(key_scales[:], key_scale_pool[:].indirect(list1[:]))
         kept_grouped = sb.tile([P, J, PACK], BF16, name="kept_grouped", align_bytes=64)
-        nc.vector.tensor_copy(kept_grouped[:].rearrange("p (c i) j -> p c j i", i=4),
-                              kept_picked[:].rearrange("p j (c i) -> p c j i", i=4))
+        for t, copy in enumerate((nc.vector.tensor_copy, nc.scalar.copy)):
+            copy(kept_grouped[:, t * P:(t + 1) * P, :].rearrange("p (c i) j -> p c j i", i=4),
+                 kept_picked[:, :, t * P:(t + 1) * P].rearrange("p j (c i) -> p c j i", i=4))
         kept_codes = sb.tile([P, J], U32, name="kept_codes", align_bytes=64)
         kept_scales = sb.tile([P, J], U8, name="kept_scales", align_bytes=64)
         quantize(kept_codes[:], kept_scales[:], kept_grouped[:].rearrange("p c j -> p (c j)"))
+
+        query_grouped = sb.tile([P, Q, PACK], BF16, name="query_grouped", tag="load4", align_bytes=64)
+        query_codes = sb.tile([P, Q], U32, name="query_codes", align_bytes=64)
+        query_scales = sb.tile([P, Q], U8, name="query_scales", align_bytes=64)
+        nc.vector.tensor_copy(query_grouped[:].rearrange("p (c i) j -> p c j i", i=4),
+                              query_raw[:].rearrange("p j (c i) -> p c j i", i=4))
+        quantize(query_codes[:], query_scales[:], query_grouped[:].rearrange("p c j -> p (c j)"))
+
         val_pool = []
 
         def load_values(e, tag):
-            val_pool.append(sb.tile([P, T], F32, name=f"val_pool{e}", tag=tag))
+            val_pool.append(sb.tile([P, T], F32, name=f"val_pool{e}", tag=tag, align_bytes=64))
             nc.sync.dma_start(val_pool[e][:], vals[e * P:(e + 1) * P, :])
 
-        for e in range(2):
-            load_values(e, f"load{e}")
+        for e, tag in enumerate(("load0", "load1", "load2", "load4")):
+            load_values(e, tag)
 
         key_words = sb.tile([P, I], U32, name="key_words", align_bytes=64)
         for h in range(2):
             nc.vector.tensor_copy(key_words[:, h * HALF:(h + 1) * HALF],
                                   key_word_pool[:].indirect(list1[:, h * (HALF // LANES):(h + 1) * (HALF // LANES)]))
-        load_values(2, "load3")
         m1_cols = sb.tile([P, I // P], F32, name="m1_cols")
         kk, largest = [], []
         for h in range(2):
@@ -144,7 +134,6 @@ def tile_attend_novel_typical_comparedrows_kernel(
             nc.scalar.activation(first[:], kk[h][:, 0, :], ACT.Copy, scale=cols[:, 2:3])
             largest.append(sb.tile([P, HALF], F32, name=f"largest{h}", tag=f"largest{h}"))
             nc.vector.scalar_tensor_tensor(largest[h][:], kk[h][:, 1, :], cols[:, 3:4], first[:], ALU.mult, ALU.max)
-        load_values(3, "first1")
         for h in range(2):
             turned = bank(f"b{h}", [P, 2, P], f"turned{h}")
             for t in range(2):
@@ -168,20 +157,24 @@ def tile_attend_novel_typical_comparedrows_kernel(
         for t in range(2):
             minus_s.append(sb.tile([P, I], F32, name=f"minus_s{t}"))
             s_sum.append(sb.tile([P, 1], F32, name=f"s_sum{t}"))
-            nc.vector.scalar_tensor_tensor(minus_s[t][:], m1_rows[:], late_cols[:, t:t + 1], a0[t][:],
+            nc.vector.scalar_tensor_tensor(minus_s[t][:], m1_rows[:], cols[:, 4 + t:5 + t], a0[t][:],
                                            ALU.mult, ALU.subtract, accum_out=s_sum[t][:])
+        late_t = bank("b4", [P, P], "late_t")
+        nc.tensor.transpose(late_t[:], late_rows[:], ident[:])
+        late_cols = sb.tile([P, 6], F32, name="late_cols")
+        nc.vector.tensor_copy(late_cols[:], late_t[:, 0:6])
+        os_rows = bank("b5", [P, I], "os_rows")
+        for t in range(I // P):
+            nc.tensor.transpose(os_rows[:, t * P:(t + 1) * P], late_cols[:, t:t + 1].to_broadcast([P, P]), ident[:])
         for t in range(2):
             square = sb.tile([P, I], F32, name=f"square{t}", tag=f"square{t}")
             nc.scalar.activation(square[:], minus_s[t][:], ACT.Square, scale=-float(I), bias=s_sum[t][:])
             root.append(sb.tile([P, I], F32, name=f"root{t}", tag=f"root{t}"))
-            nc.scalar.activation(root[t][:], square[:], ACT.Abs_reciprocal_sqrt, scale=square_scale[:, t:t + 1], bias=1.0)
+            nc.scalar.activation(root[t][:], square[:], ACT.Abs_reciprocal_sqrt, scale=cols[:, t:t + 1], bias=1.0)
         for t in range(2):
             part = sb.tile([P, I], F32, name=f"part{t}", tag=f"part{t}")
             part_sum = sb.tile([P, 1], F32, name=f"part_sum{t}")
-            if t == 0:
-                nc.vector.scalar_tensor_tensor(part[:], root[t][:], 1.0, root[t][:], ALU.mult, ALU.mult, accum_out=part_sum[:])
-            else:
-                nc.scalar.activation(part[:], root[t][:], ACT.Square, accum_out=part_sum[:])
+            nc.scalar.activation(part[:], root[t][:], ACT.Square, accum_out=part_sum[:])
             inv_sum = sb.tile([P, 1], F32, name=f"inv_sum{t}")
             nc.vector.reciprocal(inv_sum[:], part_sum[:])
             weight = sb.tile([P, I], BF16, name=f"weight{t}")
@@ -191,18 +184,23 @@ def tile_attend_novel_typical_comparedrows_kernel(
             for u in range(2):
                 nc.tensor.transpose(weight_t[:, u, :], words[:, u:I // 2:2], ident[:])
             rows_t_cols = slice(t * P, (t + 1) * P)
-            leave_bank = nc.scalar.copy if t == 0 else nc.vector.tensor_copy
-            leave_bank(weight_grouped[:, rows_t_cols, :].bitcast(F32), weight_t[:].rearrange("p u q -> p q u"))
+            nc.vector.tensor_copy(weight_grouped[:, rows_t_cols, :].bitcast(F32), weight_t[:].rearrange("p u q -> p q u"))
             quantize(weight_codes[:, rows_t_cols], weight_scales[:, rows_t_cols],
                      weight_grouped[:, rows_t_cols, :].rearrange("p c j -> p (c j)"))
 
+        hold_bank = bank("b1", [P, Q], "hold_bank")
+        for t in range(Q // P):
+            nc.tensor.transpose(hold_bank[:, t * P:(t + 1) * P], late_cols[:, 4 + t:5 + t].to_broadcast([P, P]), ident[:])
+        hold_rows = sb.tile([P, Q], F32, name="hold_rows")
+        nc.vector.tensor_copy(hold_rows[:], hold_bank[:])
+
         val_codes, val_scales = [], []
         for e in range(E // P):
-            picked = sb.tile([P, I], BF16, name=f"val_picked{e}", tag=("largest1", "a0_1", "root1", "part1")[e])
-            if e == 0:
+            picked = sb.tile([P, I], BF16, name=f"val_picked{e}", tag=("largest1", "a0_0", "a0_1", "part1")[e])
+            if e == 3:
                 nc.scalar.activation(picked[:, :HALF], val_pool[e][:].indirect(list1[:, :HALF // LANES]), ACT.Copy)
                 nc.vector.tensor_copy(picked[:, HALF:], val_pool[e][:].indirect(list1[:, HALF // LANES:]))
-            elif e == 1:
+            elif e > 0:
                 nc.vector.tensor_copy(picked[:], val_pool[e][:].indirect(list1[:]))
             else:
                 nc.scalar.activation(picked[:], val_pool[e][:].indirect(list1[:]), ACT.Copy)
@@ -223,8 +221,8 @@ def tile_attend_novel_typical_comparedrows_kernel(
             nc.gpsimd.memset(o_window[:, Q:], 0.0)
             nc.scalar.copy(o_window[:, :Q], o_bank[:])
             taken = sb.tile([P, Q], F32, name=f"taken{e}")
-            if e == 2:
-                named = sb.tile([P, Q], F32, name="named")
+            if e % 2 == 1:
+                named = sb.tile([P, Q], F32, name=f"named{e}")
                 nc.scalar.activation(named[:], o_window[:].indirect(list3[:]), ACT.Copy)
                 nc.vector.tensor_tensor(taken[:], named[:], hold_rows[:], ALU.mult)
             else:

@@ -63,17 +63,17 @@ def tile_attend_novel_typical_comparedrows_kernel(
             nc.sync.dma_start(key_scale_pool[r:P:32, :].bitcast(I32), keys_scales[0, r:16:4, :].bitcast(I32))
         nc.sync.dma_start(rows[2:4, :], kw1.rearrange("o (t p) -> t (o p)", t=2))
         nc.sync.dma_start(rows[4:6, :], lam.rearrange("o (t p) -> t (o p)", t=2))
-        root_rows = sb.tile([2, P], F32, name="root_rows", tag="load2", align_bytes=64)
+        root_rows = sb.tile([2, P], F32, name="root_rows", tag="load3", align_bytes=64)
         nc.scalar.activation(root_rows[:], width_rows[:], ACT.Abs_reciprocal_sqrt)
-        inverse_rows = sb.tile([2, P], F32, name="inverse_rows", tag="load3")
+        inverse_rows = sb.tile([2, P], F32, name="inverse_rows", tag="load2", align_bytes=64)
         nc.scalar.activation(inverse_rows[:], root_rows[:], ACT.Square)
         nc.scalar.activation(rows[0:2, :], inverse_rows[:], ACT.Square, scale=1.0 / I)
         kept_pool.append(sb.tile([P, 2, U], F32, name="kept_pool1", tag="load1", align_bytes=64))
         nc.sync.dma_start(kept_pool[1][:], kept_planes[:, 2:4, :])
+        key_word_pool = sb.tile([P, T], U32, name="key_word_pool", tag="load3", align_bytes=64)
+        nc.sync.dma_start(key_word_pool[:].bitcast(I32), keys_words[0].rearrange("p n t -> p (n t)").bitcast(I32))
         query_raw = sb.tile([P, PACK, Q], F32, name="query_raw", tag="load2", align_bytes=64)
         nc.sync.dma_start(query_raw[:], query.rearrange("(p j) q -> p j q", j=PACK))
-        key_word_pool = sb.tile([P, T], U32, name="key_word_pool", tag="load3")
-        nc.sync.dma_start(key_word_pool[:].bitcast(I32), keys_words[0].rearrange("p n t -> p (n t)").bitcast(I32))
 
         rows_t = bank("b0", [P, P], "rows_t")
         nc.tensor.transpose(rows_t[:], rows[:], ident[:])
@@ -101,20 +101,13 @@ def tile_attend_novel_typical_comparedrows_kernel(
         kept_scales = sb.tile([P, J], U8, name="kept_scales", align_bytes=64)
         quantize(kept_codes[:], kept_scales[:], kept_grouped[:].rearrange("p c j -> p (c j)"))
 
-        query_grouped = sb.tile([P, Q, PACK], BF16, name="query_grouped", tag="load4", align_bytes=64)
-        query_codes = sb.tile([P, Q], U32, name="query_codes", align_bytes=64)
-        query_scales = sb.tile([P, Q], U8, name="query_scales", align_bytes=64)
-        nc.vector.tensor_copy(query_grouped[:].rearrange("p (c i) j -> p c j i", i=4),
-                              query_raw[:].rearrange("p j (c i) -> p c j i", i=4))
-        quantize(query_codes[:], query_scales[:], query_grouped[:].rearrange("p c j -> p (c j)"))
-
         val_pool = []
 
         def load_values(e, tag):
             val_pool.append(sb.tile([P, T], F32, name=f"val_pool{e}", tag=tag, align_bytes=64))
             nc.sync.dma_start(val_pool[e][:], vals[e * P:(e + 1) * P, :])
 
-        for e, tag in enumerate(("load0", "load1", "load2", "load4")):
+        for e, tag in enumerate(("load0", "load1", "load4")):
             load_values(e, tag)
 
         key_words = sb.tile([P, I], U32, name="key_words", align_bytes=64)
@@ -129,22 +122,42 @@ def tile_attend_novel_typical_comparedrows_kernel(
             for t in range(2):
                 mx(kk[h][:, t, :], kept_codes[:, t * P:(t + 1) * P], kept_scales[:, t * P:(t + 1) * P],
                    key_words[:, slots], key_scales[:, slots])
+        query_grouped = sb.tile([P, Q, PACK], BF16, name="query_grouped", tag="load3", align_bytes=64)
+        query_codes = sb.tile([P, Q], U32, name="query_codes", align_bytes=64)
+        query_scales = sb.tile([P, Q], U8, name="query_scales", align_bytes=64)
+        nc.vector.tensor_copy(query_grouped[:].rearrange("p (c i) j -> p c j i", i=4),
+                              query_raw[:].rearrange("p j (c i) -> p c j i", i=4))
+        load_values(3, "load2")
         for h in range(2):
             first = sb.tile([P, HALF], F32, name=f"first{h}", tag=f"first{h}")
             nc.scalar.activation(first[:], kk[h][:, 0, :], ACT.Copy, scale=cols[:, 2:3])
-            largest.append(sb.tile([P, HALF], F32, name=f"largest{h}", tag=f"largest{h}"))
+            largest.append(sb.tile([P, HALF], F32, name=f"largest{h}", tag=f"largest{h}", align_bytes=64))
             nc.vector.scalar_tensor_tensor(largest[h][:], kk[h][:, 1, :], cols[:, 3:4], first[:], ALU.mult, ALU.max)
+        quantize(query_codes[:], query_scales[:], query_grouped[:].rearrange("p c j -> p (c j)"))
         for h in range(2):
             turned = bank(f"b{h}", [P, 2, P], f"turned{h}")
             for t in range(2):
                 nc.tensor.transpose(turned[:, t, :], largest[h][:, t * P:(t + 1) * P], ident[:])
             nc.vector.tensor_reduce(m1_cols[:, 2 * h:2 * h + 2], turned[:], AXIS.X, ALU.max)
-        a0 = []
+        late_t = bank("b0", [P, P], "late_t")
+        nc.tensor.transpose(late_t[:], late_rows[:], ident[:])
+        late_cols = sb.tile([P, 6], F32, name="late_cols")
+        nc.vector.tensor_copy(late_cols[:], late_t[:, 0:6])
+        val_picked = []
+
+        def pick_values(e, tag, on_vector):
+            val_picked.append(sb.tile([P, I], BF16, name=f"val_picked{e}", tag=tag, align_bytes=64))
+            if on_vector:
+                nc.vector.tensor_copy(val_picked[e][:], val_pool[e][:].indirect(list1[:]))
+            else:
+                nc.scalar.activation(val_picked[e][:], val_pool[e][:].indirect(list1[:]), ACT.Copy)
+
+        pick_values(0, "largest1", True)
+        a0 = sb.tile([P, 2, I], F32, name="a0", tag="a0", align_bytes=64)
         for t in range(2):
             a0_bank = bank(f"b{2 + t}", [P, I], f"a0_bank{t}")
             mx(a0_bank[:], query_codes[:, t * P:(t + 1) * P], query_scales[:, t * P:(t + 1) * P], key_words[:], key_scales[:])
-            a0.append(sb.tile([P, I], F32, name=f"a0_{t}", tag=f"a0_{t}"))
-            nc.scalar.copy(a0[t][:], a0_bank[:])
+            nc.scalar.copy(a0[:, t, :], a0_bank[:])
         m1_rows = bank("b4", [P, I], "m1_rows")
         for t in range(I // P):
             nc.tensor.transpose(m1_rows[:, t * P:(t + 1) * P], m1_cols[:, t:t + 1].to_broadcast([P, P]), ident[:])
@@ -155,27 +168,25 @@ def tile_attend_novel_typical_comparedrows_kernel(
         weight_scales = sb.tile([P, Q], U8, name="weight_scales", align_bytes=64)
         minus_s, s_sum, root = [], [], []
         for t in range(2):
-            minus_s.append(sb.tile([P, I], F32, name=f"minus_s{t}"))
+            minus_s.append(sb.tile([P, I], F32, name=f"minus_s{t}", tag=("load0", "minus_s1")[t], align_bytes=64))
             s_sum.append(sb.tile([P, 1], F32, name=f"s_sum{t}"))
-            nc.vector.scalar_tensor_tensor(minus_s[t][:], m1_rows[:], cols[:, 4 + t:5 + t], a0[t][:],
+            nc.vector.scalar_tensor_tensor(minus_s[t][:], m1_rows[:], cols[:, 4 + t:5 + t], a0[:, t, :],
                                            ALU.mult, ALU.subtract, accum_out=s_sum[t][:])
-        late_t = bank("b4", [P, P], "late_t")
-        nc.tensor.transpose(late_t[:], late_rows[:], ident[:])
-        late_cols = sb.tile([P, 6], F32, name="late_cols")
-        nc.vector.tensor_copy(late_cols[:], late_t[:, 0:6])
-        os_rows = bank("b5", [P, I], "os_rows")
+        os_rows = bank("b4", [P, I], "os_rows")
         for t in range(I // P):
             nc.tensor.transpose(os_rows[:, t * P:(t + 1) * P], late_cols[:, t:t + 1].to_broadcast([P, P]), ident[:])
+        pick_values(1, "a0", True)
+        pick_values(2, "largest0", True)
         for t in range(2):
             square = sb.tile([P, I], F32, name=f"square{t}", tag=f"square{t}")
             nc.scalar.activation(square[:], minus_s[t][:], ACT.Square, scale=-float(I), bias=s_sum[t][:])
-            root.append(sb.tile([P, I], F32, name=f"root{t}", tag=f"root{t}"))
+            root.append(sb.tile([P, I], F32, name=f"root{t}", tag=f"root{t}", align_bytes=64))
             nc.scalar.activation(root[t][:], square[:], ACT.Abs_reciprocal_sqrt, scale=cols[:, t:t + 1], bias=1.0)
         for t in range(2):
-            part = sb.tile([P, I], F32, name=f"part{t}", tag=f"part{t}")
+            part = sb.tile([P, I], F32, name=f"part{t}", tag=f"part{t}", align_bytes=64)
             part_sum = sb.tile([P, 1], F32, name=f"part_sum{t}")
             nc.scalar.activation(part[:], root[t][:], ACT.Square, accum_out=part_sum[:])
-            inv_sum = sb.tile([P, 1], F32, name=f"inv_sum{t}")
+            inv_sum = sb.tile([P, 1], F32, name=f"inv_sum{t}", tag=("load4", "inv_sum1")[t], align_bytes=64)
             nc.vector.reciprocal(inv_sum[:], part_sum[:])
             weight = sb.tile([P, I], BF16, name=f"weight{t}")
             nc.vector.scalar_tensor_tensor(weight[:], part[:], inv_sum[:], os_rows[:], ALU.mult, ALU.mult)
@@ -188,37 +199,32 @@ def tile_attend_novel_typical_comparedrows_kernel(
             quantize(weight_codes[:, rows_t_cols], weight_scales[:, rows_t_cols],
                      weight_grouped[:, rows_t_cols, :].rearrange("p c j -> p (c j)"))
 
-        hold_bank = bank("b1", [P, Q], "hold_bank")
+        pick_values(3, "root1", False)
+        hold_bank = bank("b2", [P, Q], "hold_bank")
         for t in range(Q // P):
             nc.tensor.transpose(hold_bank[:, t * P:(t + 1) * P], late_cols[:, 4 + t:5 + t].to_broadcast([P, P]), ident[:])
         hold_rows = sb.tile([P, Q], F32, name="hold_rows")
-        nc.vector.tensor_copy(hold_rows[:], hold_bank[:])
+        nc.scalar.copy(hold_rows[:], hold_bank[:])
 
         val_codes, val_scales = [], []
         for e in range(E // P):
-            picked = sb.tile([P, I], BF16, name=f"val_picked{e}", tag=("largest1", "a0_0", "a0_1", "part1")[e])
-            if e == 3:
-                nc.scalar.activation(picked[:, :HALF], val_pool[e][:].indirect(list1[:, :HALF // LANES]), ACT.Copy)
-                nc.vector.tensor_copy(picked[:, HALF:], val_pool[e][:].indirect(list1[:, HALF // LANES:]))
-            elif e > 0:
-                nc.vector.tensor_copy(picked[:], val_pool[e][:].indirect(list1[:]))
-            else:
-                nc.scalar.activation(picked[:], val_pool[e][:].indirect(list1[:]), ACT.Copy)
             val_t = bank(f"b{6 + e % 2}", [P, 2, P], f"val_t{e}")
-            words = picked[:].bitcast(F32)
+            words = val_picked[e][:].bitcast(F32)
             for u in range(2):
                 nc.tensor.transpose(val_t[:, u, :], words[:, u:I // 2:2], ident[:])
-            grouped = sb.tile([P, P, PACK], BF16, name=f"val_grouped{e}", align_bytes=64)
-            nc.scalar.copy(grouped[:].bitcast(F32), val_t[:].rearrange("p u c -> p c u"))
+            grouped = sb.tile([P, P, PACK], BF16, name=f"val_grouped{e}", align_bytes=64,
+                              tag=("val_grouped0", "part1", "inv_sum1", "val_grouped3")[e])
+            leave_bank = nc.vector.tensor_copy if e in (1, 2) else nc.scalar.copy
+            leave_bank(grouped[:].bitcast(F32), val_t[:].rearrange("p u c -> p c u"))
             val_codes.append(sb.tile([P, P], U32, name=f"val_codes{e}", align_bytes=64))
             val_scales.append(sb.tile([P, P], U8, name=f"val_scales{e}", align_bytes=64))
             quantize(val_codes[e][:], val_scales[e][:], grouped[:].rearrange("p c j -> p (c j)"))
 
         for e in range(E // P):
-            o_bank = bank(("b2", "b3", "b4", "b0")[e], [P, Q], f"o_bank{e}")
+            o_bank = bank(("b5", "b3", "b1", "b0")[e], [P, Q], f"o_bank{e}")
             mx(o_bank[:], val_codes[e][:], val_scales[e][:], weight_codes[:], weight_scales[:])
-            o_window = sb.tile([P, Q + SPARE], F32, name=f"o_window{e}")
-            nc.gpsimd.memset(o_window[:, Q:], 0.0)
+            o_window = sb.tile([P, Q + SPARE], F32, name=f"o_window{e}", tag=("load2", "o1", "o2", "o3")[e], align_bytes=64)
+            (nc.vector if e == 0 else nc.gpsimd).memset(o_window[:, Q:], 0.0)
             nc.scalar.copy(o_window[:, :Q], o_bank[:])
             taken = sb.tile([P, Q], F32, name=f"taken{e}")
             if e % 2 == 1:

from contextlib import ExitStack

import concourse.mybir as mybir
from concourse.masks import make_identity

D, T, I, Q, E, J, U = 512, 2048, 512, 256, 512, 256, 1024
FLOPS = 2 * D * I * Q + 2 * D * I * J + 2 * I * E * Q

F32 = mybir.dt.float32
BF16 = mybir.dt.bfloat16
I32 = mybir.dt.int32
U32 = mybir.dt.uint32
U16 = mybir.dt.uint16
U8 = mybir.dt.uint8
FP8X4 = mybir.dt.float8_e4m3fn_x4
ALU = mybir.AluOpType
ACT = mybir.ActivationFunctionType
AXIS = mybir.AxisListType

P = 128
PACK = 4
LANES = 16
HALF = I // 2
SPARE = 16


def tile_attend_novel_typical_comparedrows_kernel(
    tc, query, keys_words, keys_scales, kept, kw1, lam, width, slot_factor, vals, hold, offs, offs2, offs3, out
):
    nc = tc.nc
    with ExitStack() as ctx:
        sb = ctx.enter_context(tc.tile_pool(name="sb", bufs=1))
        ps = ctx.enter_context(tc.psum_pool(name="ps", bufs=1))

        def bank(tag, shape, name):
            return ps.tile(shape, F32, tag=tag, name=name)

        def mx(out_ap, lhs, lhs_sc, rhs, rhs_sc):
            nc.tensor.matmul_mx(out=out_ap, lhsT=lhs.bitcast(FP8X4), lhsT_scale=lhs_sc,
                                rhs=rhs.bitcast(FP8X4), rhs_scale=rhs_sc, start=True, stop=True)

        def quantize(codes, scales, grouped):
            nc.vector.quantize_mx(out=codes.bitcast(FP8X4), scales=scales, in_=grouped)

        key_scale_pool = sb.tile([P, T], U8, name="key_scale_pool")
        nc.gpsimd.memset(key_scale_pool[:].bitcast(I32), 0)
        rows = sb.tile([P, P], F32, name="rows", tag="late")
        nc.gpsimd.memset(rows[:], 0.0)
        ident = sb.tile([P, P], F32, name="ident")
        make_identity(nc, ident[:])
        list2 = sb.tile([P, J // LANES], U16, name="list2")
        list1 = sb.tile([P, I // LANES], U16, name="list1")
        list3 = sb.tile([P, Q // LANES], U16, name="list3")
        width_rows = sb.tile([2, P], F32, name="width_rows", tag="load1", align_bytes=64)
        kept_planes = kept.rearrange("(p j) u -> p j u", j=PACK)
        kept_pool = [sb.tile([P, 2, U], F32, name="kept_pool0", tag="load0", align_bytes=64)]
        nc.sync.dma_start(list2[:], offs2)
        nc.scalar.dma_start(width_rows[:], width.rearrange("(t p) o -> t (p o)", t=2))
        nc.sync.dma_start(list1[:], offs)
        nc.sync.dma_start(list3[:], offs3)
        nc.sync.dma_start(kept_pool[0][:], kept_planes[:, 0:2, :])
        for r in range(4):
            nc.sync.dma_start(key_scale_pool[r:P:32, :].bitcast(I32), keys_scales[0, r:16:4, :].bitcast(I32))
        nc.sync.dma_start(rows[2:4, :], kw1.rearrange("o (t p) -> t (o p)", t=2))
        nc.sync.dma_start(rows[4:6, :], lam.rearrange("o (t p) -> t (o p)", t=2))
        root_rows = sb.tile([2, P], F32, name="root_rows", tag="load3", align_bytes=64)
        nc.scalar.activation(root_rows[:], width_rows[:], ACT.Abs_reciprocal_sqrt)
        inverse_rows = sb.tile([2, P], F32, name="inverse_rows", tag="load2", align_bytes=64)
        nc.scalar.activation(inverse_rows[:], root_rows[:], ACT.Square)
        nc.scalar.activation(rows[0:2, :], inverse_rows[:], ACT.Square, scale=1.0 / I)
        kept_pool.append(sb.tile([P, 2, U], F32, name="kept_pool1", tag="load1", align_bytes=64))
        nc.sync.dma_start(kept_pool[1][:], kept_planes[:, 2:4, :])
        key_word_pool = sb.tile([P, T], U32, name="key_word_pool", tag="load3", align_bytes=64)
        nc.sync.dma_start(key_word_pool[:].bitcast(I32), keys_words[0].rearrange("p n t -> p (n t)").bitcast(I32))
        query_raw = sb.tile([P, PACK, Q], F32, name="query_raw", tag="load2", align_bytes=64)
        nc.sync.dma_start(query_raw[:], query.rearrange("(p j) q -> p j q", j=PACK))

        rows_t = bank("b0", [P, P], "rows_t")
        nc.tensor.transpose(rows_t[:], rows[:], ident[:])
        late_rows = sb.tile([P, P], F32, name="late_rows", tag="late")
        nc.gpsimd.memset(late_rows[:], 0.0)
        nc.sync.dma_start(late_rows[0:4, :], slot_factor.rearrange("o (t p) -> t (o p)", t=4))
        nc.sync.dma_start(late_rows[4:6, :], hold.rearrange("o (t p) -> t (o p)", t=2))
        cols = sb.tile([P, 6], F32, name="cols")
        nc.scalar.copy(cols[:], rows_t[:, 0:6])

        kept_picked = sb.tile([P, PACK, J], F32, name="kept_picked", tag="load4", align_bytes=64)
        for j in range(PACK):
            window = kept_pool[j // 2][:, j % 2, :].indirect(list2[:])
            if j % 2 == 0:
                nc.scalar.activation(kept_picked[:, j, :], window, ACT.Copy)
            else:
                nc.vector.tensor_copy(kept_picked[:, j, :], window)
        key_scales = sb.tile([P, I], U8, name="key_scales", align_bytes=64)
        nc.vector.tensor_copy(key_scales[:], key_scale_pool[:].indirect(list1[:]))
        kept_grouped = sb.tile([P, J, PACK], BF16, name="kept_grouped", align_bytes=64)
        for t, copy in enumerate((nc.vector.tensor_copy, nc.scalar.copy)):
            copy(kept_grouped[:, t * P:(t + 1) * P, :].rearrange("p (c i) j -> p c j i", i=4),
                 kept_picked[:, :, t * P:(t + 1) * P].rearrange("p j (c i) -> p c j i", i=4))
        kept_codes = sb.tile([P, J], U32, name="kept_codes", align_bytes=64)
        kept_scales = sb.tile([P, J], U8, name="kept_scales", align_bytes=64)
        quantize(kept_codes[:], kept_scales[:], kept_grouped[:].rearrange("p c j -> p (c j)"))

        val_pool = []

        def load_values(e, tag):
            val_pool.append(sb.tile([P, T], F32, name=f"val_pool{e}", tag=tag, align_bytes=64))
            nc.sync.dma_start(val_pool[e][:], vals[e * P:(e + 1) * P, :])

        for e, tag in enumerate(("load0", "load1", "load4")):
            load_values(e, tag)

        key_words = sb.tile([P, I], U32, name="key_words", align_bytes=64)
        for h in range(2):
            nc.vector.tensor_copy(key_words[:, h * HALF:(h + 1) * HALF],
                                  key_word_pool[:].indirect(list1[:, h * (HALF // LANES):(h + 1) * (HALF // LANES)]))
        m1_cols = sb.tile([P, I // P], F32, name="m1_cols")
        kk, largest = [], []
        for h in range(2):
            slots = slice(h * HALF, (h + 1) * HALF)
            kk.append(bank(f"b{h}", [P, 2, HALF], f"kk{h}"))
            for t in range(2):
                mx(kk[h][:, t, :], kept_codes[:, t * P:(t + 1) * P], kept_scales[:, t * P:(t + 1) * P],
                   key_words[:, slots], key_scales[:, slots])
        query_grouped = sb.tile([P, Q, PACK], BF16, name="query_grouped", tag="load3", align_bytes=64)
        query_codes = sb.tile([P, Q], U32, name="query_codes", align_bytes=64)
        query_scales = sb.tile([P, Q], U8, name="query_scales", align_bytes=64)
        nc.vector.tensor_copy(query_grouped[:].rearrange("p (c i) j -> p c j i", i=4),
                              query_raw[:].rearrange("p j (c i) -> p c j i", i=4))
        load_values(3, "load2")
        for h in range(2):
            first = sb.tile([P, HALF], F32, name=f"first{h}", tag=f"first{h}")
            nc.scalar.activation(first[:], kk[h][:, 0, :], ACT.Copy, scale=cols[:, 2:3])
            largest.append(sb.tile([P, HALF], F32, name=f"largest{h}", tag=f"largest{h}", align_bytes=64))
            nc.vector.scalar_tensor_tensor(largest[h][:], kk[h][:, 1, :], cols[:, 3:4], first[:], ALU.mult, ALU.max)
        quantize(query_codes[:], query_scales[:], query_grouped[:].rearrange("p c j -> p (c j)"))
        for h in range(2):
            turned = bank(f"b{h}", [P, 2, P], f"turned{h}")
            for t in range(2):
                nc.tensor.transpose(turned[:, t, :], largest[h][:, t * P:(t + 1) * P], ident[:])
            nc.vector.tensor_reduce(m1_cols[:, 2 * h:2 * h + 2], turned[:], AXIS.X, ALU.max)
        late_t = bank("b0", [P, P], "late_t")
        nc.tensor.transpose(late_t[:], late_rows[:], ident[:])
        late_cols = sb.tile([P, 6], F32, name="late_cols")
        nc.vector.tensor_copy(late_cols[:], late_t[:, 0:6])
        val_picked = []

        def pick_values(e, tag, on_vector):
            val_picked.append(sb.tile([P, I], BF16, name=f"val_picked{e}", tag=tag, align_bytes=64))
            if on_vector:
                nc.vector.tensor_copy(val_picked[e][:], val_pool[e][:].indirect(list1[:]))
            else:
                nc.scalar.activation(val_picked[e][:], val_pool[e][:].indirect(list1[:]), ACT.Copy)

        pick_values(0, "largest1", True)
        a0 = sb.tile([P, 2, I], F32, name="a0", tag="a0", align_bytes=64)
        for t in range(2):
            a0_bank = bank(f"b{2 + t}", [P, I], f"a0_bank{t}")
            mx(a0_bank[:], query_codes[:, t * P:(t + 1) * P], query_scales[:, t * P:(t + 1) * P], key_words[:], key_scales[:])
            nc.scalar.copy(a0[:, t, :], a0_bank[:])
        m1_rows = bank("b4", [P, I], "m1_rows")
        for t in range(I // P):
            nc.tensor.transpose(m1_rows[:, t * P:(t + 1) * P], m1_cols[:, t:t + 1].to_broadcast([P, P]), ident[:])


        weight_grouped = sb.tile([P, Q, PACK], BF16, name="weight_grouped", align_bytes=64)
        weight_codes = sb.tile([P, Q], U32, name="weight_codes", align_bytes=64)
        weight_scales = sb.tile([P, Q], U8, name="weight_scales", align_bytes=64)
        minus_s, s_sum, root = [], [], []
        for t in range(2):
            minus_s.append(sb.tile([P, I], F32, name=f"minus_s{t}", tag=("load0", "minus_s1")[t], align_bytes=64))
            s_sum.append(sb.tile([P, 1], F32, name=f"s_sum{t}"))
            nc.vector.scalar_tensor_tensor(minus_s[t][:], m1_rows[:], cols[:, 4 + t:5 + t], a0[:, t, :],
                                           ALU.mult, ALU.subtract, accum_out=s_sum[t][:])
        os_rows = bank("b4", [P, I], "os_rows")
        for t in range(I // P):
            nc.tensor.transpose(os_rows[:, t * P:(t + 1) * P], late_cols[:, t:t + 1].to_broadcast([P, P]), ident[:])
        pick_values(1, "a0", True)
        pick_values(2, "largest0", True)
        for t in range(2):
            square = sb.tile([P, I], F32, name=f"square{t}", tag=f"square{t}")
            nc.scalar.activation(square[:], minus_s[t][:], ACT.Square, scale=-float(I), bias=s_sum[t][:])
            root.append(sb.tile([P, I], F32, name=f"root{t}", tag=f"root{t}", align_bytes=64))
            nc.scalar.activation(root[t][:], square[:], ACT.Abs_reciprocal_sqrt, scale=cols[:, t:t + 1], bias=1.0)
        for t in range(2):
            part = sb.tile([P, I], F32, name=f"part{t}", tag=f"part{t}", align_bytes=64)
            part_sum = sb.tile([P, 1], F32, name=f"part_sum{t}")
            nc.scalar.activation(part[:], root[t][:], ACT.Square, accum_out=part_sum[:])
            inv_sum = sb.tile([P, 1], F32, name=f"inv_sum{t}", tag=("load4", "inv_sum1")[t], align_bytes=64)
            nc.vector.reciprocal(inv_sum[:], part_sum[:])
            weight = sb.tile([P, I], BF16, name=f"weight{t}")
            nc.vector.scalar_tensor_tensor(weight[:], part[:], inv_sum[:], os_rows[:], ALU.mult, ALU.mult)
            weight_t = bank(f"b{2 + t}", [P, 2, P], f"weight_t{t}")
            words = weight[:].bitcast(F32)
            for u in range(2):
                nc.tensor.transpose(weight_t[:, u, :], words[:, u:I // 2:2], ident[:])
            rows_t_cols = slice(t * P, (t + 1) * P)
            nc.vector.tensor_copy(weight_grouped[:, rows_t_cols, :].bitcast(F32), weight_t[:].rearrange("p u q -> p q u"))
            quantize(weight_codes[:, rows_t_cols], weight_scales[:, rows_t_cols],
                     weight_grouped[:, rows_t_cols, :].rearrange("p c j -> p (c j)"))

        pick_values(3, "root1", False)
        hold_bank = bank("b2", [P, Q], "hold_bank")
        for t in range(Q // P):
            nc.tensor.transpose(hold_bank[:, t * P:(t + 1) * P], late_cols[:, 4 + t:5 + t].to_broadcast([P, P]), ident[:])
        hold_rows = sb.tile([P, Q], F32, name="hold_rows")
        nc.scalar.copy(hold_rows[:], hold_bank[:])

        val_codes, val_scales = [], []
        for e in range(E // P):
            val_t = bank(f"b{6 + e % 2}", [P, 2, P], f"val_t{e}")
            words = val_picked[e][:].bitcast(F32)
            for u in range(2):
                nc.tensor.transpose(val_t[:, u, :], words[:, u:I // 2:2], ident[:])
            grouped = sb.tile([P, P, PACK], BF16, name=f"val_grouped{e}", align_bytes=64,
                              tag=("val_grouped0", "part1", "inv_sum1", "val_grouped3")[e])
            leave_bank = nc.vector.tensor_copy if e in (1, 2) else nc.scalar.copy
            leave_bank(grouped[:].bitcast(F32), val_t[:].rearrange("p u c -> p c u"))
            val_codes.append(sb.tile([P, P], U32, name=f"val_codes{e}", align_bytes=64))
            val_scales.append(sb.tile([P, P], U8, name=f"val_scales{e}", align_bytes=64))
            quantize(val_codes[e][:], val_scales[e][:], grouped[:].rearrange("p c j -> p (c j)"))

        for e in range(E // P):
            o_bank = bank(("b5", "b3", "b1", "b0")[e], [P, Q], f"o_bank{e}")
            mx(o_bank[:], val_codes[e][:], val_scales[e][:], weight_codes[:], weight_scales[:])
            o_window = sb.tile([P, Q + SPARE], F32, name=f"o_window{e}", tag=("load2", "o1", "o2", "o3")[e], align_bytes=64)
            (nc.vector if e == 0 else nc.gpsimd).memset(o_window[:, Q:], 0.0)
            nc.scalar.copy(o_window[:, :Q], o_bank[:])
            taken = sb.tile([P, Q], F32, name=f"taken{e}")
            if e % 2 == 1:
                named = sb.tile([P, Q], F32, name=f"named{e}")
                nc.scalar.activation(named[:], o_window[:].indirect(list3[:]), ACT.Copy)
                nc.vector.tensor_tensor(taken[:], named[:], hold_rows[:], ALU.mult)
            else:
                nc.vector.tensor_tensor(taken[:], o_window[:].indirect(list3[:]), hold_rows[:], ALU.mult)
            result = sb.tile([P, Q], F32, name=f"result{e}")
            nc.vector.tensor_tensor(result[:], o_bank[:], taken[:], ALU.subtract)
            nc.sync.dma_start(out[e * P:(e + 1) * P, :], result[:])
